import numpy as np
import ml_dtypes


def mxq(x, axis, fmt="e4m3"):
    dtype, down = {"e4m3": (ml_dtypes.float8_e4m3fn, 7), "e5m2": (ml_dtypes.float8_e5m2, 14)}[fmt]
    v = np.moveaxis(np.asarray(x, np.float32).astype(ml_dtypes.bfloat16).astype(np.float64), axis, -1)
    blocks = v.reshape(v.shape[:-1] + (-1, 32))
    amax = np.abs(blocks).max(-1, keepdims=True)
    byte = np.maximum(np.where(amax > 0, np.frexp(amax)[1] - 1 + 127, 0) - down, 1)
    scale = np.exp2(byte - 127.0)
    codes = (blocks / scale).astype(np.float32).astype(dtype).astype(np.float64)
    return np.moveaxis((codes * scale).reshape(v.shape), -1, axis)


WIDE = False


def mx_kscale(k):
    if not WIDE:
        return np.ones(k)
    levels = np.array([10, -10, 5, -5, 0])
    if k % 512:
        return np.exp2(np.random.permutation(np.resize(levels, k // 32))).repeat(32)
    a = np.empty((k // 512, 16))
    for p in range(k // 512):
        a[p, :8] = np.random.permutation(np.resize(levels, 8))
        for g in range(8):
            far = levels[np.abs(levels - a[p, g]) >= 10]
            a[p, g + 8] = far[np.random.randint(len(far))]
    return np.exp2(a.ravel()).repeat(32)


BF16 = ml_dtypes.bfloat16


def bf(x):
    return np.asarray(x, np.float32).astype(BF16)


def f64(x):
    return np.asarray(x).astype(np.float64)


E2M1 = np.array([0.0, 0.5, 1.0, 1.5, 2.0, 3.0, 4.0, 6.0, -0.0, -0.5, -1.0, -1.5, -2.0, -3.0, -4.0, -6.0])


def pack_weight(w, fmt):
    k, n = w.shape
    w = f64(bf(w)).reshape(k // 32, 32, n)
    amax = np.abs(w).max(1)
    if fmt == "e4m3":
        byte = np.frexp(amax)[1] - 1 + 127 - 7
    else:
        mant, ex = np.frexp(amax / 6.0)
        byte = np.where(mant > 0.5, ex, ex - 1) + 127
    byte = np.clip(np.where(amax > 0, byte, 1), 1, 254)
    scaled = (w * np.exp2(127.0 - byte)[:, None, :]).reshape(k, n).astype(np.float32)
    by_word = np.ascontiguousarray(scaled.reshape(k // 512, 128, 4, n).transpose(0, 1, 3, 2))
    if fmt == "e4m3":
        words = by_word.astype(ml_dtypes.float8_e4m3fn).view(np.uint8)
    else:
        c = by_word.astype(ml_dtypes.float4_e2m1fn).view(np.uint8) & 0xF
        words = c[..., 0::2] | (c[..., 1::2] << 4)
    return np.ascontiguousarray(words), np.ascontiguousarray(byte.astype(np.uint8).reshape(k // 512, 16, n))


def unpack_weight(words, scales, fmt):
    g, p, n, _ = words.shape
    if fmt == "e4m3":
        vals = np.ascontiguousarray(words).view(ml_dtypes.float8_e4m3fn).astype(np.float64)
    else:
        nib = np.empty((g, p, n, 4), np.uint8)
        nib[..., 0::2] = words & 0xF
        nib[..., 1::2] = words >> 4
        vals = E2M1[nib]
    vals = vals * np.repeat(np.exp2(scales.astype(np.float64) - 127.0), 8, axis=1)[..., None]
    return vals.transpose(0, 1, 3, 2).reshape(g * 512, n)
def pack4(w):
    words, scales = pack_weight(w, "e2m1")
    return words.reshape(words.shape[0], 128, -1), scales


def unpack4(words, scales):
    return unpack_weight(words.reshape(words.shape[0], 128, -1, 2), scales, "e2m1")


def planes(Y):
    n, m = Y.shape
    b = f64(bf(Y)).reshape(n // 32, 32, m)
    amax = np.abs(b).max(1)
    byte = np.clip(np.where(amax > 0, np.frexp(amax)[1] - 1 + 127 - 7, 1), 1, 254)
    codes = (b * np.exp2(127.0 - byte)[:, None, :]).reshape(n, m).astype(np.float32).astype(ml_dtypes.float8_e4m3fn).view(np.uint8)
    words = codes.reshape(n // 512, 128, 4, m).transpose(0, 1, 3, 2)
    return np.ascontiguousarray(words), np.ascontiguousarray(byte.astype(np.uint8).reshape(n // 512, 16, m))


M, K, N = 768, 1536, 1024

SPREAD = 0.8
TILT = 2.0


def draw_factor(v, tilt):
    return (np.random.randn(K, N) + tilt * v[:, None] / np.sqrt(K)) / np.sqrt(K)


def setup_inputs():
    s = mx_kscale(K)
    v = np.sign(np.random.randn(K))
    x = 0.8 * np.random.randn(M, K) + 0.6 * v[None, :]
    l = draw_factor(v, TILT) * np.exp(SPREAD * np.random.randn(N))[None, :]
    r = draw_factor(v, TILT)
    b = 0.7 * draw_factor(v, 0.0)
    z = np.random.randn(M, N)
    x_words, x_scales = pack_weight((x * s[None, :]).T, "e4m3")
    l_words, l_scales = pack4(l / s[:, None])
    r_words, r_scales = pack_weight(r / s[:, None], "e4m3")
    return {"x_words": x_words, "x_scales": x_scales,
            "l_words": l_words, "l_scales": l_scales,
            "r_words": r_words, "r_scales": r_scales,
            "b": bf(b / s[:, None]), "z": bf(z)}


def reference(x_words, x_scales, l_words, l_scales, r_words, r_scales, b, z):
    X = unpack_weight(x_words, x_scales, "e4m3").T
    L = unpack4(l_words, l_scales)
    R = unpack_weight(r_words, r_scales, "e4m3")
    B = mxq(f64(b), 0, "e4m3")
    left = X @ L
    right = X @ R
    fit = X @ B
    e = f64(z) - fit
    y = (left * right) * e ** 2
    Y = y.T
    words, scales = planes(Y)
    return y, words, scales

@@ -1,0 +1,272 @@
+from contextlib import ExitStack
+
+import concourse.mybir as mybir
+from concourse.masks import make_identity
+
+M, K, N = 768, 1536, 1024
+FLOPS = 3 * 2 * M * K * N
+
+F32 = mybir.dt.float32
+BF16 = mybir.dt.bfloat16
+I32 = mybir.dt.int32
+U32 = mybir.dt.uint32
+U8 = mybir.dt.uint8
+FP8X4 = mybir.dt.float8_e4m3fn_x4
+FP4X4 = mybir.dt.float4_e2m1fn_x4
+ALU = mybir.AluOpType
+ACT = mybir.ActivationFunctionType
+
+P = 128
+PACK = 4
+KP = P * PACK
+G = K // KP
+W = 512
+H = N // W
+MT = M // P
+R_ROW = 4
+V_COLS = 344
+
+
+def tile_cook_numerator_scores_k3_kernel(tc, x_words, x_scales, l_words, l_scales, r_words, r_scales, b, z, out_0, out_1, out_2):
+    nc = tc.nc
+    with ExitStack() as ctx:
+        sb = ctx.enter_context(tc.tile_pool(name="sb", bufs=1))
+        ps = ctx.enter_context(tc.psum_pool(name="ps", bufs=1))
+
+        def tile(name, shape, dtype):
+            return sb.tile(shape, dtype, name=name, align_bytes=64)
+
+        bank = [ps.tile([P, W], F32, name="bank%d" % i) for i in range(8)]
+        ident = tile("ident", [P, P], F32)
+        xw = [tile("xw%d" % g, [P, M], U32) for g in range(G)]
+        xs = tile("xs", [P, G, M], U8)
+        lw = [tile("lw%d" % h, [P, G, 2 * W], U8) for h in range(H)]
+        ls = tile("ls", [P, G, N], U8)
+        rw = [tile("rw%d" % h, [P, G, W], U32) for h in range(H)]
+        rs = tile("rs", [P, G, N], U8)
+        braw = [[tile("braw%d%d" % (h, g), [P, PACK, W], BF16) for g in range(G)] for h in range(H)]
+        bgrp = [[tile("bgrp%d%d" % (h, g), [P, W, PACK], BF16) for g in range(G)] for h in range(H)]
+        bw = [[tile("bw%d%d" % (h, g), [P, W], U32) for g in range(G)] for h in range(H)]
+        bs = [[tile("bs%d%d" % (h, g), [P, W], U8) for g in range(G)] for h in range(H)]
+        zt = [[tile("zt%d%d" % (h, c), [P, 3, W], BF16) for c in range(2)] for h in range(H)]
+        res = [tile("res%d" % i, [P, W], F32) for i in range(3)]
+        sq = [tile("sq%d" % m, [P, W], F32) for m in range(MT)]
+        part = [tile("part%d" % m, [P, W], F32) for m in range(MT)]
+        y = [[tile("y%d%d" % (h, m), [P, W], F32) for m in range(MT)] for h in range(H)]
+        ybf = [[tile("ybf%d%d" % (h, m), [P, W], BF16) for m in range(MT)] for h in range(H)]
+        yt = [[tile("yt%d%d" % (h, c), [P, 2 * W], BF16) for c in range(MT // 2)] for h in range(H)]
+        yw = [tile("yw%d" % h, [P, M], U32) for h in range(H)]
+        ys = [tile("ys%d" % h, [P, M], U8) for h in range(H)]
+
+        def cols(h):
+            return slice(h * W, (h + 1) * W)
+
+        def rows(m):
+            return slice(m * P, (m + 1) * P)
+
+        def load_scales(plane, src, row0):
+            for q in range(4):
+                nc.sync.dma_start(out=plane[32 * q + row0 : 32 * q + row0 + 4, :, :].bitcast(I32),
+                                  in_=src[:, 4 * q : 4 * q + 4, :].rearrange("g r n -> r g n").bitcast(I32))
+
+        def load_b(h, g):
+            nc.sync.dma_start(out=braw[h][g][:], in_=b[g * KP : (g + 1) * KP, cols(h)].rearrange("(p j) n -> p j n", j=PACK))
+
+        def load_x(g):
+            nc.sync.dma_start(out=xw[g][:].bitcast(I32), in_=x_words[g].rearrange("p m t -> p (m t)").bitcast(I32))
+
+        def load_l(h):
+            nc.sync.dma_start(out=lw[h][:].bitcast(I32),
+                              in_=l_words[:, :, 2 * W * h : 2 * W * (h + 1)].rearrange("g p n -> p g n").bitcast(I32))
+
+        def load_r(h):
+            nc.sync.dma_start(out=rw[h][:].bitcast(I32),
+                              in_=r_words[:, :, cols(h), :].rearrange("g p n t -> p g (n t)").bitcast(I32))
+
+        def load_z(h, c):
+            nc.sync.dma_start(out=zt[h][c][:], in_=z[3 * P * c : 3 * P * (c + 1), cols(h)].rearrange("(m p) n -> p m n", p=P))
+
+        def interleave(copy, h, g, c0, c1):
+            copy(out=bgrp[h][g][:, c0:c1, :].rearrange("p (c i) t -> p c t i", i=4),
+                 in_=braw[h][g][:, :, c0:c1].rearrange("p t (c i) -> p c t i", i=4))
+
+        def quantize_b(h, g):
+            nc.vector.quantize_mx(out=bw[h][g][:].bitcast(FP8X4), scales=bs[h][g][:],
+                                  in_=bgrp[h][g][:].rearrange("p n t -> p (n t)"))
+
+        def mx_pass(acc, m, g, words, scale):
+            nc.tensor.matmul_mx(out=acc[:], lhsT=xw[g][:, rows(m)].bitcast(FP8X4), lhsT_scale=xs[:, g, rows(m)],
+                                rhs=words, rhs_scale=scale, start=(g == 0), stop=(g == G - 1))
+
+        def fit_pass(acc, h, m, g):
+            mx_pass(acc, m, g, bw[h][g][:].bitcast(FP8X4), bs[h][g][:])
+
+        def fit(acc, h, m):
+            for g in range(G):
+                fit_pass(acc, h, m, g)
+
+        def left(acc, h, m):
+            for g in range(G):
+                mx_pass(acc, m, g, lw[h][:, g, :].bitcast(FP4X4), ls[:, g, cols(h)])
+
+        def right(acc, h, m):
+            for g in range(G):
+                mx_pass(acc, m, g, rw[h][:, g, :].bitcast(FP8X4), rs[R_ROW:P, g, cols(h)])
+
+        def residual(acc, h, m):
+            nc.vector.tensor_tensor(out=res[m % 3][:], in0=zt[h][m // 3][:, m % 3, :], in1=acc[:], op=ALU.subtract)
+            nc.scalar.activation(out=sq[m][:], in_=res[m % 3][:], func=ACT.Square)
+
+        def times_left(acc, m):
+            nc.vector.tensor_tensor(out=part[m][:], in0=acc[:], in1=sq[m][:], op=ALU.mult)
+
+        def times_right(acc, h, m):
+            nc.vector.tensor_tensor(out=y[h][m][:], in0=acc[:], in1=part[m][:], op=ALU.mult)
+            nc.sync.dma_start(out=out_0[rows(m), cols(h)], in_=y[h][m][:])
+
+        def round_y(copy, h, m):
+            copy(out=ybf[h][m][:].rearrange("m (u p e) -> m u p e", u=2, e=2),
+                 in_=y[h][m][:].rearrange("m (p u e) -> m u p e", u=2, e=2))
+
+        def turn(acc, h, m):
+            words = ybf[h][m][:].bitcast(F32)
+            for u in range(2):
+                j = 2 * (m % 2) + u
+                nc.tensor.transpose(acc[:, j * P : (j + 1) * P], words[:, u * P : (u + 1) * P], ident[:])
+
+        def gather(copy, acc, h, m0, m1):
+            i0, i1 = m0 % 2, (m1 - 1) % 2 + 1
+            copy(out=yt[h][m0 // 2][:].bitcast(F32).rearrange("p (i r u) -> p i r u", i=2, u=2)[:, i0:i1],
+                 in_=acc[:].rearrange("p (i u r) -> p i r u", i=2, u=2)[:, i0:i1])
+
+        def quantize_y(h, m0, m1):
+            i0, i1 = m0 % 2, (m1 - 1) % 2 + 1
+            nc.vector.quantize_mx(out=yw[h][:, m0 * P : m1 * P].bitcast(FP8X4), scales=ys[h][:, m0 * P : m1 * P],
+                                  in_=yt[h][m0 // 2][:, i0 * W : i1 * W])
+
+        def store_planes(queues, h, m0, m1):
+            span = slice(m0 * P, m1 * P)
+            queues[0].dma_start(out=out_1[h, :, span, :].rearrange("p m t -> p (m t)").bitcast(I32), in_=yw[h][:, span].bitcast(I32))
+            for q in range(4):
+                queues[(q + 1) % len(queues)].dma_start(out=out_2[h, 4 * q : 4 * q + 4, span].bitcast(I32),
+                                                        in_=ys[h][32 * q : 32 * q + 4, span].bitcast(I32))
+
+        vcopy, scopy = nc.vector.tensor_copy, nc.scalar.copy
+
+        with tc.manual_schedule():
+            for plane in (xs, ls, rs):
+                nc.vector.memset(plane[:].rearrange("p g n -> p (g n)").bitcast(I32), 0)
+            make_identity(nc, ident[:])
+
+            load_b(0, 0)
+            load_scales(xs, x_scales, 0)
+            load_x(0)
+            for g in range(1, G):
+                load_b(0, g)
+                load_x(g)
+            load_scales(ls, l_scales, 0)
+            load_l(0)
+            load_z(0, 0)
+            load_z(0, 1)
+            load_b(1, 0)
+            load_scales(rs, r_scales, R_ROW)
+            load_r(0)
+            load_b(1, 1)
+            load_b(1, 2)
+            load_l(1)
+            load_r(1)
+            load_z(1, 0)
+            load_z(1, 1)
+
+            for g in range(G):
+                interleave(vcopy, 0, g, 0, V_COLS)
+                interleave(scopy, 0, g, V_COLS, W)
+                quantize_b(0, g)
+                for m in range(MT):
+                    fit_pass(bank[m], 0, m, g)
+
+            for m in range(MT):
+                residual(bank[m], 0, m)
+                if m >= 2:
+                    times_left(bank[(m + 4) % 8], m - 2)
+                left(bank[(m + 6) % 8], 0, m)
+                if m >= 2:
+                    interleave(scopy, 1, 0, 128 * (m - 2), 128 * (m - 1))
+            for m in range(MT - 2, MT):
+                times_left(bank[(m + 6) % 8], m)
+            quantize_b(1, 0)
+
+            interleave(scopy, 1, 1, 0, W)
+            interleave(scopy, 1, 2, 0, W)
+            for m in range(MT):
+                right(bank[(m + 4) % 8], 0, m)
+                times_right(bank[(m + 4) % 8], 0, m)
+                if m == 3:
+                    quantize_b(1, 1)
+            quantize_b(1, 2)
+
+            lb, rb, fb, tb = bank[2:4], bank[4:6], bank[6:8], bank[0:2]
+            left(lb[0], 1, 0)
+            right(rb[0], 1, 0)
+            fit(fb[0], 1, 0)
+            residual(fb[0], 1, 0)
+            for m in range(MT):
+                if m > 0:
+                    left(lb[m % 2], 1, m)
+                if m == 0:
+                    fit(fb[1], 1, 1)
+                    residual(fb[1], 1, 1)
+                times_left(lb[m % 2], m)
+                if 0 < m < MT - 1:
+                    fit(fb[(m + 1) % 2], 1, m + 1)
+                    residual(fb[(m + 1) % 2], 1, m + 1)
+                if m > 0:
+                    right(rb[m % 2], 1, m)
+                if m == 0:
+                    round_y(vcopy, 0, 0)
+                if m == 2:
+                    quantize_y(0, 0, 2)
+                    quantize_y(0, 2, 4)
+                if m == 4:
+                    quantize_y(0, 4, 6)
+                    quantize_y(1, 0, 2)
+                    store_planes([nc.sync], 0, 0, MT)
+                if m == 5:
+                    quantize_y(1, 2, 4)
+                    store_planes([nc.sync], 1, 0, 4)
+                times_right(rb[m % 2], 1, m)
+                if m == 0:
+                    for mm in range(1, 4):
+                        round_y(scopy, 0, mm)
+                if m == 1:
+                    for mm in range(4):
+                        turn(tb[mm // 2], 0, mm)
+                    gather(scopy, tb[0], 0, 0, 2)
+                    gather(scopy, tb[1], 0, 2, 4)
+                    round_y(scopy, 0, 4)
+                if m == 2:
+                    round_y(scopy, 0, 5)
+                    round_y(scopy, 1, 0)
+                    round_y(scopy, 1, 1)
+                if m == 3:
+                    turn(tb[0], 0, 4)
+                    turn(tb[0], 0, 5)
+                    turn(tb[1], 1, 0)
+                    turn(tb[1], 1, 1)
+                    gather(scopy, tb[0], 0, 4, 6)
+                    gather(scopy, tb[1], 1, 0, 2)
+                    round_y(scopy, 1, 2)
+                    round_y(scopy, 1, 3)
+                if m == 4:
+                    turn(tb[0], 1, 2)
+                    turn(tb[0], 1, 3)
+                    gather(scopy, tb[0], 1, 2, 4)
+                    round_y(scopy, 1, 4)
+            turn(tb[1], 1, 4)
+            gather(scopy, tb[1], 1, 4, 5)
+            round_y(vcopy, 1, 5)
+            quantize_y(1, 4, 5)
+            turn(tb[0], 1, 5)
+            gather(scopy, tb[0], 1, 5, 6)
+            quantize_y(1, 5, 6)
+            store_planes([nc.sync, nc.scalar], 1, 4, MT)

@@ -24,7 +24,8 @@ W = 512
 H = N // W
 MT = M // P
 R_ROW = 4
-V_COLS = 344
+V_COLS = 144
+WARM_PASSES = 28
 
 
 def tile_cook_numerator_scores_k3_kernel(tc, x_words, x_scales, l_words, l_scales, r_words, r_scales, b, z, out_0, out_1, out_2):
@@ -58,16 +59,19 @@ def tile_cook_numerator_scores_k3_kernel(tc, x_words, x_scales, l_words, l_scale
         yw = [tile("yw%d" % h, [P, M], U32) for h in range(H)]
         ys = [tile("ys%d" % h, [P, M], U8) for h in range(H)]
 
+        ones = tile("ones", [P, W], BF16)
+        onew = tile("onew", [P, P], U32)
+        ones_s = tile("ones_s", [P, P], U8)
+
         def cols(h):
             return slice(h * W, (h + 1) * W)
 
         def rows(m):
             return slice(m * P, (m + 1) * P)
 
-        def load_scales(plane, src, row0):
-            for q in range(4):
-                nc.sync.dma_start(out=plane[32 * q + row0 : 32 * q + row0 + 4, :, :].bitcast(I32),
-                                  in_=src[:, 4 * q : 4 * q + 4, :].rearrange("g r n -> r g n").bitcast(I32))
+        def load_scales(plane, src, row0, r, span):
+            nc.sync.dma_start(out=plane[row0 + r : P : 32, :, span].bitcast(I32),
+                              in_=src.rearrange("g (q r) n -> r q g n", r=4)[r][:, :, span].bitcast(I32))
 
         def load_b(h, g):
             nc.sync.dma_start(out=braw[h][g][:], in_=b[g * KP : (g + 1) * KP, cols(h)].rearrange("(p j) n -> p j n", j=PACK))
@@ -90,9 +94,9 @@ def tile_cook_numerator_scores_k3_kernel(tc, x_words, x_scales, l_words, l_scale
             copy(out=bgrp[h][g][:, c0:c1, :].rearrange("p (c i) t -> p c t i", i=4),
                  in_=braw[h][g][:, :, c0:c1].rearrange("p t (c i) -> p c t i", i=4))
 
-        def quantize_b(h, g):
-            nc.vector.quantize_mx(out=bw[h][g][:].bitcast(FP8X4), scales=bs[h][g][:],
-                                  in_=bgrp[h][g][:].rearrange("p n t -> p (n t)"))
+        def quantize_b(h, g, c0=0, c1=W):
+            nc.vector.quantize_mx(out=bw[h][g][:, c0:c1].bitcast(FP8X4), scales=bs[h][g][:, c0:c1],
+                                  in_=bgrp[h][g][:, c0:c1, :].rearrange("p n t -> p (n t)"))
 
         def mx_pass(acc, m, g, words, scale):
             nc.tensor.matmul_mx(out=acc[:], lhsT=xw[g][:, rows(m)].bitcast(FP8X4), lhsT_scale=xs[:, g, rows(m)],
@@ -144,110 +148,129 @@ def tile_cook_numerator_scores_k3_kernel(tc, x_words, x_scales, l_words, l_scale
             nc.vector.quantize_mx(out=yw[h][:, m0 * P : m1 * P].bitcast(FP8X4), scales=ys[h][:, m0 * P : m1 * P],
                                   in_=yt[h][m0 // 2][:, i0 * W : i1 * W])
 
-        def store_planes(queues, h, m0, m1):
+        def store_planes(queues, h, m0, m1, with_scales):
             span = slice(m0 * P, m1 * P)
             queues[0].dma_start(out=out_1[h, :, span, :].rearrange("p m t -> p (m t)").bitcast(I32), in_=yw[h][:, span].bitcast(I32))
-            for q in range(4):
-                queues[(q + 1) % len(queues)].dma_start(out=out_2[h, 4 * q : 4 * q + 4, span].bitcast(I32),
-                                                        in_=ys[h][32 * q : 32 * q + 4, span].bitcast(I32))
+            if with_scales:
+                for q in range(4):
+                    queues[(q + 1) % len(queues)].dma_start(out=out_2[h, 4 * q : 4 * q + 4, :].bitcast(I32),
+                                                            in_=ys[h][32 * q : 32 * q + 4, :].bitcast(I32))
 
         vcopy, scopy = nc.vector.tensor_copy, nc.scalar.copy
 
         with tc.manual_schedule():
-            for plane in (xs, ls, rs):
-                nc.vector.memset(plane[:].rearrange("p g n -> p (g n)").bitcast(I32), 0)
+            nc.vector.memset(xs[:].rearrange("p g n -> p (g n)").bitcast(I32), 0)
+            nc.vector.memset(ones[:], 1.0)
+            nc.vector.memset(ls[:].rearrange("p g n -> p (g n)").bitcast(I32), 0)
+            nc.vector.quantize_mx(out=onew[:].bitcast(FP8X4), scales=ones_s[:], in_=ones[:])
+            nc.vector.memset(rs[:].rearrange("p g n -> p (g n)").bitcast(I32), 0)
+            for i in range(WARM_PASSES):
+                nc.tensor.matmul_mx(out=bank[7][:, 0:P], lhsT=onew[:].bitcast(FP8X4), lhsT_scale=ones_s[:],
+                                    rhs=onew[:].bitcast(FP8X4), rhs_scale=ones_s[:], start=True, stop=True)
             make_identity(nc, ident[:])
 
             load_b(0, 0)
-            load_scales(xs, x_scales, 0)
+            for r in range(4):
+                load_scales(xs, x_scales, 0, r, slice(0, M))
             load_x(0)
             for g in range(1, G):
                 load_b(0, g)
                 load_x(g)
-            load_scales(ls, l_scales, 0)
+            for r in range(4):
+                load_scales(ls, l_scales, 0, r, slice(0, N))
             load_l(0)
             load_z(0, 0)
             load_z(0, 1)
-            load_b(1, 0)
-            load_scales(rs, r_scales, R_ROW)
+            for r in range(4):
+                load_scales(rs, r_scales, R_ROW, r, slice(0, N))
             load_r(0)
-            load_b(1, 1)
-            load_b(1, 2)
+            for g in range(G):
+                load_b(1, g)
             load_l(1)
             load_r(1)
             load_z(1, 0)
             load_z(1, 1)
 
             for g in range(G):
-                interleave(vcopy, 0, g, 0, V_COLS)
-                interleave(scopy, 0, g, V_COLS, W)
-                quantize_b(0, g)
+                for c0 in (0, W // 2):
+                    interleave(vcopy, 0, g, c0, c0 + V_COLS)
+                    interleave(scopy, 0, g, c0 + V_COLS, c0 + W // 2)
+                for c0 in (0, W // 2):
+                    quantize_b(0, g, c0, c0 + W // 2)
                 for m in range(MT):
                     fit_pass(bank[m], 0, m, g)
 
             for m in range(MT):
+                if m == MT - 1:
+                    interleave(scopy, 1, 0, 0, W // 2)
                 residual(bank[m], 0, m)
                 if m >= 2:
                     times_left(bank[(m + 4) % 8], m - 2)
                 left(bank[(m + 6) % 8], 0, m)
-                if m >= 2:
-                    interleave(scopy, 1, 0, 128 * (m - 2), 128 * (m - 1))
             for m in range(MT - 2, MT):
                 times_left(bank[(m + 6) % 8], m)
-            quantize_b(1, 0)
 
+            interleave(scopy, 1, 0, W // 2, W)
             interleave(scopy, 1, 1, 0, W)
-            interleave(scopy, 1, 2, 0, W)
+            interleave(scopy, 1, 2, V_COLS, W)
             for m in range(MT):
                 right(bank[(m + 4) % 8], 0, m)
+            for m in range(4):
                 times_right(bank[(m + 4) % 8], 0, m)
-                if m == 3:
-                    quantize_b(1, 1)
+                if m == 1:
+                    quantize_b(1, 0)
+            interleave(vcopy, 1, 2, 0, V_COLS)
+            quantize_b(1, 1)
+            times_right(bank[0], 0, 4)
             quantize_b(1, 2)
+            times_right(bank[1], 0, 5)
+            for mm in range(3):
+                round_y(scopy, 0, mm)
 
             lb, rb, fb, tb = bank[2:4], bank[4:6], bank[6:8], bank[0:2]
             left(lb[0], 1, 0)
             right(rb[0], 1, 0)
-            fit(fb[0], 1, 0)
-            residual(fb[0], 1, 0)
-            for m in range(MT):
-                if m > 0:
-                    left(lb[m % 2], 1, m)
-                if m == 0:
-                    fit(fb[1], 1, 1)
-                    residual(fb[1], 1, 1)
-                times_left(lb[m % 2], m)
-                if 0 < m < MT - 1:
-                    fit(fb[(m + 1) % 2], 1, m + 1)
-                    residual(fb[(m + 1) % 2], 1, m + 1)
-                if m > 0:
-                    right(rb[m % 2], 1, m)
-                if m == 0:
-                    round_y(vcopy, 0, 0)
+            left(lb[1], 1, 1)
+            for m in range(3):
+                fit(fb[m % 2], 1, m)
                 if m == 2:
+                    times_left(lb[0], 0)
+                residual(fb[m % 2], 1, m)
+                round_y(scopy, 0, 3 + m)
+            times_right(rb[0], 1, 0)
+            times_left(lb[1], 1)
+            right(rb[1], 1, 1)
+            round_y(vcopy, 1, 0)
+            times_right(rb[1], 1, 1)
+            for mm in range(4):
+                turn(tb[mm // 2], 0, mm)
+            gather(scopy, tb[0], 0, 0, 2)
+            for m in range(2, MT):
+                left(lb[m % 2], 1, m)
+                times_left(lb[m % 2], m)
+                if m == 2:
+                    round_y(vcopy, 1, 1)
+                if m == 3:
                     quantize_y(0, 0, 2)
-                    quantize_y(0, 2, 4)
                 if m == 4:
                     quantize_y(0, 4, 6)
+                    store_planes([nc.sync], 0, 0, MT, True)
+                if m < MT - 1:
+                    fit(fb[(m + 1) % 2], 1, m + 1)
+                    residual(fb[(m + 1) % 2], 1, m + 1)
+                    right(rb[m % 2], 1, m)
+                if m == 2:
+                    gather(scopy, tb[1], 0, 2, 4)
+                if m == 3:
+                    quantize_y(0, 2, 4)
+                    round_y(scopy, 1, 2)
+                if m == 4:
                     quantize_y(1, 0, 2)
-                    store_planes([nc.sync], 0, 0, MT)
                 if m == 5:
                     quantize_y(1, 2, 4)
-                    store_planes([nc.sync], 1, 0, 4)
-                times_right(rb[m % 2], 1, m)
-                if m == 0:
-                    for mm in range(1, 4):
-                        round_y(scopy, 0, mm)
-                if m == 1:
-                    for mm in range(4):
-                        turn(tb[mm // 2], 0, mm)
-                    gather(scopy, tb[0], 0, 0, 2)
-                    gather(scopy, tb[1], 0, 2, 4)
-                    round_y(scopy, 0, 4)
-                if m == 2:
-                    round_y(scopy, 0, 5)
-                    round_y(scopy, 1, 0)
-                    round_y(scopy, 1, 1)
+                    store_planes([nc.sync], 1, 0, 4, False)
+                if m < MT - 1:
+                    times_right(rb[m % 2], 1, m)
                 if m == 3:
                     turn(tb[0], 0, 4)
                     turn(tb[0], 0, 5)
@@ -255,18 +278,22 @@ def tile_cook_numerator_scores_k3_kernel(tc, x_words, x_scales, l_words, l_scale
                     turn(tb[1], 1, 1)
                     gather(scopy, tb[0], 0, 4, 6)
                     gather(scopy, tb[1], 1, 0, 2)
-                    round_y(scopy, 1, 2)
                     round_y(scopy, 1, 3)
                 if m == 4:
                     turn(tb[0], 1, 2)
                     turn(tb[0], 1, 3)
                     gather(scopy, tb[0], 1, 2, 4)
                     round_y(scopy, 1, 4)
+            m = MT - 1
+            right(rb[1], 1, m)
+            nc.vector.tensor_tensor(out=ybf[1][m][:].rearrange("m (u p e) -> m u p e", u=2, e=2),
+                                    in0=rb[1][:].rearrange("m (p u e) -> m u p e", u=2, e=2),
+                                    in1=part[m][:].rearrange("m (p u e) -> m u p e", u=2, e=2), op=ALU.mult)
             turn(tb[1], 1, 4)
             gather(scopy, tb[1], 1, 4, 5)
-            round_y(vcopy, 1, 5)
-            quantize_y(1, 4, 5)
             turn(tb[0], 1, 5)
             gather(scopy, tb[0], 1, 5, 6)
+            times_right(rb[1], 1, m)
+            quantize_y(1, 4, 5)
             quantize_y(1, 5, 6)
-            store_planes([nc.sync, nc.scalar], 1, 4, MT)
+            store_planes([nc.sync, nc.scalar], 1, 4, MT, True)

@@ -35,7 +35,7 @@ def tile_cook_numerator_scores_k3_kernel(tc, x_words, x_scales, l_words, l_scale
         ps = ctx.enter_context(tc.psum_pool(name="ps", bufs=1))
 
         def tile(name, shape, dtype):
-            return sb.tile(shape, dtype, name=name, align_bytes=64)
+            return sb.tile(shape, dtype, name=name, align_bytes=256)
 
         bank = [ps.tile([P, W], F32, name="bank%d" % i) for i in range(8)]
         ident = tile("ident", [P, P], F32)
@@ -159,10 +159,10 @@ def tile_cook_numerator_scores_k3_kernel(tc, x_words, x_scales, l_words, l_scale
         vcopy, scopy = nc.vector.tensor_copy, nc.scalar.copy
 
         with tc.manual_schedule():
-            nc.vector.memset(xs[:].rearrange("p g n -> p (g n)").bitcast(I32), 0)
             nc.vector.memset(ones[:], 1.0)
-            nc.vector.memset(ls[:].rearrange("p g n -> p (g n)").bitcast(I32), 0)
+            nc.vector.memset(xs[:].rearrange("p g n -> p (g n)").bitcast(I32), 0)
             nc.vector.quantize_mx(out=onew[:].bitcast(FP8X4), scales=ones_s[:], in_=ones[:])
+            nc.vector.memset(ls[:].rearrange("p g n -> p (g n)").bitcast(I32), 0)
             nc.vector.memset(rs[:].rearrange("p g n -> p (g n)").bitcast(I32), 0)
             for i in range(WARM_PASSES):
                 nc.tensor.matmul_mx(out=bank[7][:, 0:P], lhsT=onew[:].bitcast(FP8X4), lhsT_scale=ones_s[:],

from contextlib import ExitStack

import concourse.mybir as mybir
from concourse.masks import make_identity

M, K, N = 768, 1536, 1024
FLOPS = 3 * 2 * M * K * N

F32 = mybir.dt.float32
BF16 = mybir.dt.bfloat16
I32 = mybir.dt.int32
U32 = mybir.dt.uint32
U8 = mybir.dt.uint8
FP8X4 = mybir.dt.float8_e4m3fn_x4
FP4X4 = mybir.dt.float4_e2m1fn_x4
ALU = mybir.AluOpType
ACT = mybir.ActivationFunctionType

P = 128
PACK = 4
KP = P * PACK
G = K // KP
W = 512
H = N // W
MT = M // P
R_ROW = 4
V_COLS = 144
WARM_PASSES = 28


def tile_cook_numerator_scores_k3_kernel(tc, x_words, x_scales, l_words, l_scales, r_words, r_scales, b, z, out_0, out_1, out_2):
    nc = tc.nc
    with ExitStack() as ctx:
        sb = ctx.enter_context(tc.tile_pool(name="sb", bufs=1))
        ps = ctx.enter_context(tc.psum_pool(name="ps", bufs=1))

        def tile(name, shape, dtype):
            return sb.tile(shape, dtype, name=name, align_bytes=256)

        bank = [ps.tile([P, W], F32, name="bank%d" % i) for i in range(8)]
        ident = tile("ident", [P, P], F32)
        xw = [tile("xw%d" % g, [P, M], U32) for g in range(G)]
        xs = tile("xs", [P, G, M], U8)
        lw = [tile("lw%d" % h, [P, G, 2 * W], U8) for h in range(H)]
        ls = tile("ls", [P, G, N], U8)
        rw = [tile("rw%d" % h, [P, G, W], U32) for h in range(H)]
        rs = tile("rs", [P, G, N], U8)
        braw = [[tile("braw%d%d" % (h, g), [P, PACK, W], BF16) for g in range(G)] for h in range(H)]
        bgrp = [[tile("bgrp%d%d" % (h, g), [P, W, PACK], BF16) for g in range(G)] for h in range(H)]
        bw = [[tile("bw%d%d" % (h, g), [P, W], U32) for g in range(G)] for h in range(H)]
        bs = [[tile("bs%d%d" % (h, g), [P, W], U8) for g in range(G)] for h in range(H)]
        zt = [[tile("zt%d%d" % (h, c), [P, 3, W], BF16) for c in range(2)] for h in range(H)]
        res = [tile("res%d" % i, [P, W], F32) for i in range(3)]
        sq = [tile("sq%d" % m, [P, W], F32) for m in range(MT)]
        part = [tile("part%d" % m, [P, W], F32) for m in range(MT)]
        y = [[tile("y%d%d" % (h, m), [P, W], F32) for m in range(MT)] for h in range(H)]
        ybf = [[tile("ybf%d%d" % (h, m), [P, W], BF16) for m in range(MT)] for h in range(H)]
        yt = [[tile("yt%d%d" % (h, c), [P, 2 * W], BF16) for c in range(MT // 2)] for h in range(H)]
        yw = [tile("yw%d" % h, [P, M], U32) for h in range(H)]
        ys = [tile("ys%d" % h, [P, M], U8) for h in range(H)]

        ones = tile("ones", [P, W], BF16)
        onew = tile("onew", [P, P], U32)
        ones_s = tile("ones_s", [P, P], U8)

        def cols(h):
            return slice(h * W, (h + 1) * W)

        def rows(m):
            return slice(m * P, (m + 1) * P)

        def load_scales(plane, src, row0, r, span):
            nc.sync.dma_start(out=plane[row0 + r : P : 32, :, span].bitcast(I32),
                              in_=src.rearrange("g (q r) n -> r q g n", r=4)[r][:, :, span].bitcast(I32))

        def load_b(h, g):
            nc.sync.dma_start(out=braw[h][g][:], in_=b[g * KP : (g + 1) * KP, cols(h)].rearrange("(p j) n -> p j n", j=PACK))

        def load_x(g):
            nc.sync.dma_start(out=xw[g][:].bitcast(I32), in_=x_words[g].rearrange("p m t -> p (m t)").bitcast(I32))

        def load_l(h):
            nc.sync.dma_start(out=lw[h][:].bitcast(I32),
                              in_=l_words[:, :, 2 * W * h : 2 * W * (h + 1)].rearrange("g p n -> p g n").bitcast(I32))

        def load_r(h):
            nc.sync.dma_start(out=rw[h][:].bitcast(I32),
                              in_=r_words[:, :, cols(h), :].rearrange("g p n t -> p g (n t)").bitcast(I32))

        def load_z(h, c):
            nc.sync.dma_start(out=zt[h][c][:], in_=z[3 * P * c : 3 * P * (c + 1), cols(h)].rearrange("(m p) n -> p m n", p=P))

        def interleave(copy, h, g, c0, c1):
            copy(out=bgrp[h][g][:, c0:c1, :].rearrange("p (c i) t -> p c t i", i=4),
                 in_=braw[h][g][:, :, c0:c1].rearrange("p t (c i) -> p c t i", i=4))

        def quantize_b(h, g, c0=0, c1=W):
            nc.vector.quantize_mx(out=bw[h][g][:, c0:c1].bitcast(FP8X4), scales=bs[h][g][:, c0:c1],
                                  in_=bgrp[h][g][:, c0:c1, :].rearrange("p n t -> p (n t)"))

        def mx_pass(acc, m, g, words, scale):
            nc.tensor.matmul_mx(out=acc[:], lhsT=xw[g][:, rows(m)].bitcast(FP8X4), lhsT_scale=xs[:, g, rows(m)],
                                rhs=words, rhs_scale=scale, start=(g == 0), stop=(g == G - 1))

        def fit_pass(acc, h, m, g):
            mx_pass(acc, m, g, bw[h][g][:].bitcast(FP8X4), bs[h][g][:])

        def fit(acc, h, m):
            for g in range(G):
                fit_pass(acc, h, m, g)

        def left(acc, h, m):
            for g in range(G):
                mx_pass(acc, m, g, lw[h][:, g, :].bitcast(FP4X4), ls[:, g, cols(h)])

        def right(acc, h, m):
            for g in range(G):
                mx_pass(acc, m, g, rw[h][:, g, :].bitcast(FP8X4), rs[R_ROW:P, g, cols(h)])

        def residual(acc, h, m):
            nc.vector.tensor_tensor(out=res[m % 3][:], in0=zt[h][m // 3][:, m % 3, :], in1=acc[:], op=ALU.subtract)
            nc.scalar.activation(out=sq[m][:], in_=res[m % 3][:], func=ACT.Square)

        def times_left(acc, m):
            nc.vector.tensor_tensor(out=part[m][:], in0=acc[:], in1=sq[m][:], op=ALU.mult)

        def times_right(acc, h, m):
            nc.vector.tensor_tensor(out=y[h][m][:], in0=acc[:], in1=part[m][:], op=ALU.mult)
            nc.sync.dma_start(out=out_0[rows(m), cols(h)], in_=y[h][m][:])

        def round_y(copy, h, m):
            copy(out=ybf[h][m][:].rearrange("m (u p e) -> m u p e", u=2, e=2),
                 in_=y[h][m][:].rearrange("m (p u e) -> m u p e", u=2, e=2))

        def turn(acc, h, m):
            words = ybf[h][m][:].bitcast(F32)
            for u in range(2):
                j = 2 * (m % 2) + u
                nc.tensor.transpose(acc[:, j * P : (j + 1) * P], words[:, u * P : (u + 1) * P], ident[:])

        def gather(copy, acc, h, m0, m1):
            i0, i1 = m0 % 2, (m1 - 1) % 2 + 1
            copy(out=yt[h][m0 // 2][:].bitcast(F32).rearrange("p (i r u) -> p i r u", i=2, u=2)[:, i0:i1],
                 in_=acc[:].rearrange("p (i u r) -> p i r u", i=2, u=2)[:, i0:i1])

        def quantize_y(h, m0, m1):
            i0, i1 = m0 % 2, (m1 - 1) % 2 + 1
            nc.vector.quantize_mx(out=yw[h][:, m0 * P : m1 * P].bitcast(FP8X4), scales=ys[h][:, m0 * P : m1 * P],
                                  in_=yt[h][m0 // 2][:, i0 * W : i1 * W])

        def store_planes(queues, h, m0, m1, with_scales):
            span = slice(m0 * P, m1 * P)
            queues[0].dma_start(out=out_1[h, :, span, :].rearrange("p m t -> p (m t)").bitcast(I32), in_=yw[h][:, span].bitcast(I32))
            if with_scales:
                for q in range(4):
                    queues[(q + 1) % len(queues)].dma_start(out=out_2[h, 4 * q : 4 * q + 4, :].bitcast(I32),
                                                            in_=ys[h][32 * q : 32 * q + 4, :].bitcast(I32))

        vcopy, scopy = nc.vector.tensor_copy, nc.scalar.copy

        with tc.manual_schedule():
            nc.vector.memset(ones[:], 1.0)
            nc.vector.memset(xs[:].rearrange("p g n -> p (g n)").bitcast(I32), 0)
            nc.vector.quantize_mx(out=onew[:].bitcast(FP8X4), scales=ones_s[:], in_=ones[:])
            nc.vector.memset(ls[:].rearrange("p g n -> p (g n)").bitcast(I32), 0)
            nc.vector.memset(rs[:].rearrange("p g n -> p (g n)").bitcast(I32), 0)
            for i in range(WARM_PASSES):
                nc.tensor.matmul_mx(out=bank[7][:, 0:P], lhsT=onew[:].bitcast(FP8X4), lhsT_scale=ones_s[:],
                                    rhs=onew[:].bitcast(FP8X4), rhs_scale=ones_s[:], start=True, stop=True)
            make_identity(nc, ident[:])

            load_b(0, 0)
            for r in range(4):
                load_scales(xs, x_scales, 0, r, slice(0, M))
            load_x(0)
            for g in range(1, G):
                load_b(0, g)
                load_x(g)
            for r in range(4):
                load_scales(ls, l_scales, 0, r, slice(0, N))
            load_l(0)
            load_z(0, 0)
            load_z(0, 1)
            for r in range(4):
                load_scales(rs, r_scales, R_ROW, r, slice(0, N))
            load_r(0)
            for g in range(G):
                load_b(1, g)
            load_l(1)
            load_r(1)
            load_z(1, 0)
            load_z(1, 1)

            for g in range(G):
                for c0 in (0, W // 2):
                    interleave(vcopy, 0, g, c0, c0 + V_COLS)
                    interleave(scopy, 0, g, c0 + V_COLS, c0 + W // 2)
                for c0 in (0, W // 2):
                    quantize_b(0, g, c0, c0 + W // 2)
                for m in range(MT):
                    fit_pass(bank[m], 0, m, g)

            for m in range(MT):
                if m == MT - 1:
                    interleave(scopy, 1, 0, 0, W // 2)
                residual(bank[m], 0, m)
                if m >= 2:
                    times_left(bank[(m + 4) % 8], m - 2)
                left(bank[(m + 6) % 8], 0, m)
            for m in range(MT - 2, MT):
                times_left(bank[(m + 6) % 8], m)

            interleave(scopy, 1, 0, W // 2, W)
            interleave(scopy, 1, 1, 0, W)
            interleave(scopy, 1, 2, V_COLS, W)
            for m in range(MT):
                right(bank[(m + 4) % 8], 0, m)
            for m in range(4):
                times_right(bank[(m + 4) % 8], 0, m)
                if m == 1:
                    quantize_b(1, 0)
            interleave(vcopy, 1, 2, 0, V_COLS)
            quantize_b(1, 1)
            times_right(bank[0], 0, 4)
            quantize_b(1, 2)
            times_right(bank[1], 0, 5)
            for mm in range(3):
                round_y(scopy, 0, mm)

            lb, rb, fb, tb = bank[2:4], bank[4:6], bank[6:8], bank[0:2]
            left(lb[0], 1, 0)
            right(rb[0], 1, 0)
            left(lb[1], 1, 1)
            for m in range(3):
                fit(fb[m % 2], 1, m)
                if m == 2:
                    times_left(lb[0], 0)
                residual(fb[m % 2], 1, m)
                round_y(scopy, 0, 3 + m)
            times_right(rb[0], 1, 0)
            times_left(lb[1], 1)
            right(rb[1], 1, 1)
            round_y(vcopy, 1, 0)
            times_right(rb[1], 1, 1)
            for mm in range(4):
                turn(tb[mm // 2], 0, mm)
            gather(scopy, tb[0], 0, 0, 2)
            for m in range(2, MT):
                left(lb[m % 2], 1, m)
                times_left(lb[m % 2], m)
                if m == 2:
                    round_y(vcopy, 1, 1)
                if m == 3:
                    quantize_y(0, 0, 2)
                if m == 4:
                    quantize_y(0, 4, 6)
                    store_planes([nc.sync], 0, 0, MT, True)
                if m < MT - 1:
                    fit(fb[(m + 1) % 2], 1, m + 1)
                    residual(fb[(m + 1) % 2], 1, m + 1)
                    right(rb[m % 2], 1, m)
                if m == 2:
                    gather(scopy, tb[1], 0, 2, 4)
                if m == 3:
                    quantize_y(0, 2, 4)
                    round_y(scopy, 1, 2)
                if m == 4:
                    quantize_y(1, 0, 2)
                if m == 5:
                    quantize_y(1, 2, 4)
                    store_planes([nc.sync], 1, 0, 4, False)
                if m < MT - 1:
                    times_right(rb[m % 2], 1, m)
                if m == 3:
                    turn(tb[0], 0, 4)
                    turn(tb[0], 0, 5)
                    turn(tb[1], 1, 0)
                    turn(tb[1], 1, 1)
                    gather(scopy, tb[0], 0, 4, 6)
                    gather(scopy, tb[1], 1, 0, 2)
                    round_y(scopy, 1, 3)
                if m == 4:
                    turn(tb[0], 1, 2)
                    turn(tb[0], 1, 3)
                    gather(scopy, tb[0], 1, 2, 4)
                    round_y(scopy, 1, 4)
            m = MT - 1
            right(rb[1], 1, m)
            nc.vector.tensor_tensor(out=ybf[1][m][:].rearrange("m (u p e) -> m u p e", u=2, e=2),
                                    in0=rb[1][:].rearrange("m (p u e) -> m u p e", u=2, e=2),
                                    in1=part[m][:].rearrange("m (p u e) -> m u p e", u=2, e=2), op=ALU.mult)
            turn(tb[1], 1, 4)
            gather(scopy, tb[1], 1, 4, 5)
            turn(tb[0], 1, 5)
            gather(scopy, tb[0], 1, 5, 6)
            times_right(rb[1], 1, m)
            quantize_y(1, 4, 5)
            quantize_y(1, 5, 6)
            store_planes([nc.sync, nc.scalar], 1, 4, MT, True)
